import numpy as np
import ml_dtypes


def mxq(x, axis, fmt="e4m3"):
    dtype, down = {"e4m3": (ml_dtypes.float8_e4m3fn, 7), "e5m2": (ml_dtypes.float8_e5m2, 14)}[fmt]
    v = np.moveaxis(np.asarray(x, np.float32).astype(ml_dtypes.bfloat16).astype(np.float64), axis, -1)
    blocks = v.reshape(v.shape[:-1] + (-1, 32))
    amax = np.abs(blocks).max(-1, keepdims=True)
    byte = np.maximum(np.where(amax > 0, np.frexp(amax)[1] - 1 + 127, 0) - down, 1)
    scale = np.exp2(byte - 127.0)
    codes = (blocks / scale).astype(np.float32).astype(dtype).astype(np.float64)
    return np.moveaxis((codes * scale).reshape(v.shape), -1, axis)


WIDE = False


def mx_kscale(k):
    if not WIDE:
        return np.ones(k)
    levels = np.array([10, -10, 5, -5, 0])
    if k % 512:
        return np.exp2(np.random.permutation(np.resize(levels, k // 32))).repeat(32)
    a = np.empty((k // 512, 16))
    for p in range(k // 512):
        a[p, :8] = np.random.permutation(np.resize(levels, 8))
        for g in range(8):
            far = levels[np.abs(levels - a[p, g]) >= 10]
            a[p, g + 8] = far[np.random.randint(len(far))]
    return np.exp2(a.ravel()).repeat(32)


def f64(x):
    return np.asarray(x).astype(np.float64)


def striped8(idx):
    return np.asarray(idx).reshape(8, -1, 16).transpose(0, 2, 1).reshape(128, -1).astype(np.uint16)


def unstriped8(offs):
    return offs.reshape(8, 16, -1).transpose(0, 2, 1).reshape(8, -1).astype(np.int64)


def pick8(x, idx, run):
    r = np.arange(len(x))
    return x[r[:, None], idx[r % (8 * run) // run]]


E2M1 = np.array([0.0, 0.5, 1.0, 1.5, 2.0, 3.0, 4.0, 6.0, -0.0, -0.5, -1.0, -1.5, -2.0, -3.0, -4.0, -6.0])


def pack_weight(w, fmt):
    k, n = w.shape
    w = f64(np.asarray(w, np.float32).astype(ml_dtypes.bfloat16)).reshape(k // 32, 32, n)
    amax = np.abs(w).max(1)
    if fmt == "e4m3":
        byte = np.frexp(amax)[1] - 1 + 127 - 7
    else:
        mant, ex = np.frexp(amax / 6.0)
        byte = np.where(mant > 0.5, ex, ex - 1) + 127
    byte = np.clip(np.where(amax > 0, byte, 1), 1, 254)
    scaled = (w * np.exp2(127.0 - byte)[:, None, :]).reshape(k, n).astype(np.float32)
    by_word = np.ascontiguousarray(scaled.reshape(k // 512, 128, 4, n).transpose(0, 1, 3, 2))
    if fmt == "e4m3":
        words = by_word.astype(ml_dtypes.float8_e4m3fn).view(np.uint8)
    else:
        c = by_word.astype(ml_dtypes.float4_e2m1fn).view(np.uint8) & 0xF
        words = (c[..., 0::2] | (c[..., 1::2] << 4)).reshape(k // 512, 128, 2 * n)
    return np.ascontiguousarray(words), np.ascontiguousarray(byte.astype(np.uint8).reshape(k // 512, 16, n))


def unpack_weight(words, scales, fmt):
    g, _, n = scales.shape
    words = np.ascontiguousarray(words).reshape(g, 128, n, -1)
    if fmt == "e4m3":
        vals = words.view(ml_dtypes.float8_e4m3fn).astype(np.float64)
    else:
        nib = np.empty((g, 128, n, 4), np.uint8)
        nib[..., 0::2] = words & 0xF
        nib[..., 1::2] = words >> 4
        vals = E2M1[nib]
    vals = vals * np.repeat(np.exp2(scales.astype(np.float64) - 127.0), 8, axis=1)[..., None]
    return vals.transpose(0, 1, 3, 2).reshape(g * 512, n)


def softplus(v):
    return np.log(1.0 + np.exp(v))


D, T, I, Q = 512, 1024, 512, 128


def setup_inputs():
    n = np.random.standard_normal
    idx = np.stack([np.random.permutation(T)[:I] for _ in range(8)])
    idx2 = np.stack([np.random.permutation(T)[:I] for _ in range(8)])
    idx3 = np.stack([np.random.permutation(T)[:I] for _ in range(8)])
    fd = mx_kscale(D)
    keysp = pack_weight(n((D, T)) / fd[:, None], "e2m1")
    return {
        "query": (n((D, Q)) * 0.9 / np.sqrt(D) * fd[:, None]).astype(np.float32),
        "query2": (n((D, Q)) * 0.9 / np.sqrt(D) * fd[:, None]).astype(np.float32),
        "keys_words": keysp[0],
        "keys_scales": keysp[1],
        "lam": (np.random.uniform(1.0, 2.0, (Q, 1))).astype(np.float32),
        "old": (np.random.uniform(0.3, 1.7, (Q, T))).astype(np.float32),
        "base": (0.5 * n((Q, T))).astype(np.float32),
        "offs": striped8(idx),
        "offs2": striped8(idx2),
        "offs3": striped8(idx3),
    }


def reference(query, query2, keys_words, keys_scales, lam, old, base, offs, offs2, offs3):
    idx = unstriped8(offs)
    idx2 = unstriped8(offs2)
    idx3 = unstriped8(offs3)
    keysu = unpack_weight(keys_words, keys_scales, "e2m1")
    queryq = mxq(f64(query), 0, "e4m3")
    a = queryq.T @ keysu
    query2q = mxq(f64(query2), 0, "e4m3")
    b = query2q.T @ keysu
    ra = np.sqrt(softplus(pick8(a, idx, 16)) * softplus(pick8(b, idx, 16)) + 0.1)
    w = ra * f64(lam) - np.abs(pick8(a, idx, 16) - pick8(b, idx, 16))
    ws = w * pick8(f64(old), idx2, 16)
    f1 = np.zeros((Q, T))
    f1[np.arange(Q)[:, None], idx3[np.arange(Q) % 128 // 16]] = ws
    y = f64(base) + f1
    return y

@@ -1,0 +1,140 @@
+from contextlib import ExitStack
+
+import concourse.mybir as mybir
+
+D, T, SLOTS, Q = 512, 1024, 512, 128
+FLOPS = 2 * 2 * D * Q * T
+
+F32 = mybir.dt.float32
+BF16 = mybir.dt.bfloat16
+I32 = mybir.dt.int32
+U32 = mybir.dt.uint32
+U16 = mybir.dt.uint16
+U8 = mybir.dt.uint8
+E4M3X4 = mybir.dt.float8_e4m3fn_x4
+E2M1X4 = mybir.dt.float4_e2m1fn_x4
+ALU = mybir.AluOpType
+ACT = mybir.ActivationFunctionType
+
+P = 128
+PACK = 4
+N_MM = 256
+EXP_CAP = 2.0**60
+GATHER_CUTS = ((0, 512), (0, 256, 512))
+TAIL_CUTS = (0, 256, 512)
+N_OUT = 256
+
+
+def tile_attend_agreeingtwo_lean_timesold_heads_kernel(
+    tc, query, query2, keys_words, keys_scales, lam, old, base, offs, offs2, offs3, out
+):
+    nc = tc.nc
+    with ExitStack() as ctx:
+        sb = ctx.enter_context(tc.tile_pool(name="sb", bufs=1))
+        psum = ctx.enter_context(tc.psum_pool(name="psum", bufs=1))
+
+        k_scales = sb.tile([P, T], U8, name="k_scales", align_bytes=64)
+        nc.vector.memset(k_scales[:].bitcast(I32), 0)
+        placed = sb.tile([P, T], F32, name="placed")
+        nc.vector.memset(placed[:], 0.0)
+
+        q_raw = [sb.tile([P, PACK, Q], F32, name="q_raw%d" % i) for i in range(2)]
+        k_words = sb.tile([P, 2 * T], U8, name="k_words", align_bytes=64)
+        list_ab = sb.tile([P, SLOTS // 16], U16, name="list_ab")
+        list_old = sb.tile([P, SLOTS // 16], U16, name="list_old")
+        list_out = sb.tile([P, SLOTS // 16], U16, name="list_out")
+        old_sb = sb.tile([P, T], F32, name="old_sb")
+        base_sb = sb.tile([P, T], F32, name="base_sb")
+        lam_sb = sb.tile([P, 1], F32, name="lam_sb")
+
+        nc.sync.dma_start(out=q_raw[0][:], in_=query.rearrange("(p j) q -> p j q", j=PACK))
+        for quad in range(4):
+            nc.scalar.dma_start(
+                out=k_scales[32 * quad : 32 * quad + 4, :].bitcast(I32),
+                in_=keys_scales[0, 4 * quad : 4 * quad + 4, :].bitcast(I32),
+            )
+        nc.sync.dma_start(out=k_words[:].bitcast(I32), in_=keys_words[0].bitcast(I32))
+        nc.sync.dma_start(out=q_raw[1][:], in_=query2.rearrange("(p j) q -> p j q", j=PACK))
+        nc.sync.dma_start(list_ab[:], offs)
+        nc.sync.dma_start(out=old_sb[:], in_=old)
+        nc.sync.dma_start(list_old[:], offs2)
+        nc.sync.dma_start(list_out[:], offs3)
+        nc.sync.dma_start(out=lam_sb[:], in_=lam)
+        nc.sync.dma_start(out=base_sb[:], in_=base)
+
+        scores = []
+        for i in range(2):
+            woven = sb.tile([P, Q, PACK], BF16, name="woven%d" % i, align_bytes=64)
+            nc.vector.tensor_copy(
+                out=woven[:].rearrange("p (c i) j -> p c j i", i=4),
+                in_=q_raw[i][:].rearrange("p j (c i) -> p c j i", i=4),
+            )
+            q_codes = sb.tile([P, Q], U32, name="q_codes%d" % i, align_bytes=64)
+            q_scales = sb.tile([P, Q], U8, name="q_scales%d" % i, align_bytes=64)
+            nc.vector.quantize_mx(
+                out=q_codes[:].bitcast(E4M3X4),
+                scales=q_scales[:],
+                in_=woven[:].rearrange("p q j -> p (q j)"),
+            )
+            score = sb.tile([P, T], F32, name="score%d" % i, tag="score%d" % i)
+            for c in range(T // N_MM):
+                acc = psum.tile([P, N_MM], F32, name="acc%d_%d" % (i, c))
+                nc.tensor.matmul_mx(
+                    out=acc[:],
+                    lhsT=q_codes[:].bitcast(E4M3X4),
+                    lhsT_scale=q_scales[:],
+                    rhs=k_words[:, 2 * N_MM * c : 2 * N_MM * (c + 1)].bitcast(E2M1X4),
+                    rhs_scale=k_scales[:, N_MM * c : N_MM * (c + 1)],
+                    start=True,
+                    stop=True,
+                )
+                nc.scalar.copy(out=score[:, N_MM * c : N_MM * (c + 1)], in_=acc[:])
+            scores.append(score)
+
+        grown = sb.tile([P, 2, SLOTS], F32, name="grown")
+        picked = sb.tile([P, 2, SLOTS], F32, name="picked")
+        for i, cuts in enumerate(GATHER_CUTS):
+            for lo, hi in zip(cuts, cuts[1:]):
+                nc.vector.tensor_copy(
+                    out=picked[:, i, lo:hi], in_=scores[i][:].indirect(list_ab[:, lo // 16 : hi // 16])
+                )
+                nc.scalar.activation(out=grown[:, i, lo:hi], in_=picked[:, i, lo:hi], func=ACT.Exp)
+
+        diff = sb.tile([P, SLOTS], F32, name="diff")
+        nc.vector.tensor_tensor(out=diff[:], in0=picked[:, 0, :], in1=picked[:, 1, :], op=ALU.subtract)
+        capped = sb.tile([P, 2, SLOTS], F32, name="capped")
+        nc.vector.tensor_scalar(out=capped[:], in0=grown[:], scalar1=EXP_CAP, scalar2=None, op0=ALU.min)
+        old_picked = sb.tile([P, SLOTS], F32, name="old_picked", tag="score1")
+        nc.vector.tensor_copy(out=old_picked[:], in_=old_sb[:].indirect(list_old[:]))
+        gap = sb.tile([P, SLOTS], F32, name="gap")
+        nc.vector.scalar_tensor_tensor(
+            out=gap[:], in0=diff[:], scalar=-1.0, in1=diff[:], op0=ALU.mult, op1=ALU.max
+        )
+
+        logged = sb.tile([P, 2, SLOTS], F32, name="logged")
+        soft = sb.tile([P, 2, SLOTS], F32, name="soft")
+        for i in range(2):
+            nc.scalar.activation(out=logged[:, i, :], in_=capped[:, i, :], func=ACT.Ln, bias=1.0)
+            nc.vector.tensor_tensor(out=soft[:, i, :], in0=logged[:, i, :], in1=picked[:, i, :], op=ALU.max)
+        prod = sb.tile([P, SLOTS], F32, name="prod")
+        nc.vector.tensor_tensor(out=prod[:], in0=soft[:, 0, :], in1=soft[:, 1, :], op=ALU.mult)
+
+        root = sb.tile([P, SLOTS], F32, name="root")
+        weight = sb.tile([P, SLOTS], F32, name="weight")
+        for lo, hi in zip(TAIL_CUTS, TAIL_CUTS[1:]):
+            nc.scalar.activation(out=root[:, lo:hi], in_=prod[:, lo:hi], func=ACT.Sqrt, bias=0.1)
+            nc.vector.scalar_tensor_tensor(
+                out=weight[:, lo:hi], in0=root[:, lo:hi], scalar=lam_sb[:], in1=gap[:, lo:hi],
+                op0=ALU.mult, op1=ALU.subtract,
+            )
+            nc.vector.tensor_tensor(
+                out=placed[:].indirect(list_out[:, lo // 16 : hi // 16]),
+                in0=weight[:, lo:hi], in1=old_picked[:, lo:hi], op=ALU.mult,
+            )
+
+        for c in range(T // N_OUT):
+            cols = slice(N_OUT * c, N_OUT * (c + 1))
+            result = sb.tile([P, N_OUT], F32, name="result%d" % c)
+            nc.vector.tensor_tensor(out=result[:], in0=placed[:, cols], in1=base_sb[:, cols], op=ALU.add)
+            queue = nc.sync if c % 2 == 0 else nc.scalar
+            queue.dma_start(out=out[:, cols], in_=result[:])

@@ -20,8 +20,7 @@ P = 128
 PACK = 4
 N_MM = 256
 EXP_CAP = 2.0**60
-GATHER_CUTS = ((0, 512), (0, 256, 512))
-TAIL_CUTS = (0, 256, 512)
+HALF = SLOTS // 2
 N_OUT = 256
 
 
@@ -34,12 +33,12 @@ def tile_attend_agreeingtwo_lean_timesold_heads_kernel(
         psum = ctx.enter_context(tc.psum_pool(name="psum", bufs=1))
 
         k_scales = sb.tile([P, T], U8, name="k_scales", align_bytes=64)
-        nc.vector.memset(k_scales[:].bitcast(I32), 0)
+        nc.gpsimd.memset(k_scales[:].bitcast(I32), 0)
         placed = sb.tile([P, T], F32, name="placed")
         nc.vector.memset(placed[:], 0.0)
 
         q_raw = [sb.tile([P, PACK, Q], F32, name="q_raw%d" % i) for i in range(2)]
-        k_words = sb.tile([P, 2 * T], U8, name="k_words", align_bytes=64)
+        k_words = [sb.tile([P, T], U8, name="k_words%d" % h, tag="k_words%d" % h, align_bytes=64) for h in range(2)]
         list_ab = sb.tile([P, SLOTS // 16], U16, name="list_ab")
         list_old = sb.tile([P, SLOTS // 16], U16, name="list_old")
         list_out = sb.tile([P, SLOTS // 16], U16, name="list_out")
@@ -49,12 +48,13 @@ def tile_attend_agreeingtwo_lean_timesold_heads_kernel(
 
         nc.sync.dma_start(out=q_raw[0][:], in_=query.rearrange("(p j) q -> p j q", j=PACK))
         for quad in range(4):
-            nc.scalar.dma_start(
+            nc.sync.dma_start(
                 out=k_scales[32 * quad : 32 * quad + 4, :].bitcast(I32),
                 in_=keys_scales[0, 4 * quad : 4 * quad + 4, :].bitcast(I32),
             )
-        nc.sync.dma_start(out=k_words[:].bitcast(I32), in_=keys_words[0].bitcast(I32))
         nc.sync.dma_start(out=q_raw[1][:], in_=query2.rearrange("(p j) q -> p j q", j=PACK))
+        for h in range(2):
+            nc.sync.dma_start(out=k_words[h][:].bitcast(I32), in_=keys_words[0][:, T * h : T * (h + 1)].bitcast(I32))
         nc.sync.dma_start(list_ab[:], offs)
         nc.sync.dma_start(out=old_sb[:], in_=old)
         nc.sync.dma_start(list_old[:], offs2)
@@ -65,10 +65,13 @@ def tile_attend_agreeingtwo_lean_timesold_heads_kernel(
         scores = []
         for i in range(2):
             woven = sb.tile([P, Q, PACK], BF16, name="woven%d" % i, align_bytes=64)
-            nc.vector.tensor_copy(
-                out=woven[:].rearrange("p (c i) j -> p c j i", i=4),
-                in_=q_raw[i][:].rearrange("p j (c i) -> p c j i", i=4),
-            )
+            if i == 0:
+                nc.vector.tensor_copy(
+                    out=woven[:].rearrange("p (c i) j -> p c j i", i=4),
+                    in_=q_raw[i][:].rearrange("p j (c i) -> p c j i", i=4),
+                )
+            else:
+                nc.scalar.copy(out=woven[:], in_=q_raw[i][:].rearrange("p j q -> p q j"))
             q_codes = sb.tile([P, Q], U32, name="q_codes%d" % i, align_bytes=64)
             q_scales = sb.tile([P, Q], U8, name="q_scales%d" % i, align_bytes=64)
             nc.vector.quantize_mx(
@@ -83,7 +86,7 @@ def tile_attend_agreeingtwo_lean_timesold_heads_kernel(
                     out=acc[:],
                     lhsT=q_codes[:].bitcast(E4M3X4),
                     lhsT_scale=q_scales[:],
-                    rhs=k_words[:, 2 * N_MM * c : 2 * N_MM * (c + 1)].bitcast(E2M1X4),
+                    rhs=k_words[c // 2][:, 2 * N_MM * (c % 2) : 2 * N_MM * (c % 2 + 1)].bitcast(E2M1X4),
                     rhs_scale=k_scales[:, N_MM * c : N_MM * (c + 1)],
                     start=True,
                     stop=True,
@@ -91,45 +94,62 @@ def tile_attend_agreeingtwo_lean_timesold_heads_kernel(
                 nc.scalar.copy(out=score[:, N_MM * c : N_MM * (c + 1)], in_=acc[:])
             scores.append(score)
 
-        grown = sb.tile([P, 2, SLOTS], F32, name="grown")
-        picked = sb.tile([P, 2, SLOTS], F32, name="picked")
-        for i, cuts in enumerate(GATHER_CUTS):
-            for lo, hi in zip(cuts, cuts[1:]):
-                nc.vector.tensor_copy(
-                    out=picked[:, i, lo:hi], in_=scores[i][:].indirect(list_ab[:, lo // 16 : hi // 16])
-                )
-                nc.scalar.activation(out=grown[:, i, lo:hi], in_=picked[:, i, lo:hi], func=ACT.Exp)
+        a_all, b_all = scores
+        lo, hi = slice(0, HALF), slice(HALF, SLOTS)
+        lo_list, hi_list = slice(0, HALF // 16), slice(HALF // 16, SLOTS // 16)
+
+        a_picked = sb.tile([P, SLOTS], F32, name="a_picked")
+        b_picked = sb.tile([P, SLOTS], F32, name="b_picked")
+        nc.vector.tensor_copy(out=a_picked[:, lo], in_=a_all[:].indirect(list_ab[:, lo_list]))
+        nc.vector.tensor_copy(out=a_picked[:, hi], in_=a_all[:].indirect(list_ab[:, hi_list]))
+        nc.vector.tensor_copy(out=b_picked[:, hi], in_=b_all[:].indirect(list_ab[:, hi_list]))
+        nc.vector.tensor_copy(out=b_picked[:, lo], in_=b_all[:].indirect(list_ab[:, lo_list]))
+
+        grown = sb.tile([P, 2, SLOTS], F32, name="grown", tag="k_words1", align_bytes=64)
+        nc.scalar.activation(out=grown[:, 0, lo], in_=a_picked[:, lo], func=ACT.Exp)
+        nc.scalar.activation(out=grown[:, 1, lo], in_=b_all[:].indirect(list_ab[:, lo_list]), func=ACT.Exp)
+        nc.scalar.activation(out=grown[:, 0, hi], in_=a_picked[:, hi], func=ACT.Exp)
+        nc.scalar.activation(out=grown[:, 1, hi], in_=b_picked[:, hi], func=ACT.Exp)
 
         diff = sb.tile([P, SLOTS], F32, name="diff")
-        nc.vector.tensor_tensor(out=diff[:], in0=picked[:, 0, :], in1=picked[:, 1, :], op=ALU.subtract)
         capped = sb.tile([P, 2, SLOTS], F32, name="capped")
+        nc.vector.tensor_tensor(out=diff[:, hi], in0=a_picked[:, hi], in1=b_picked[:, hi], op=ALU.subtract)
         nc.vector.tensor_scalar(out=capped[:], in0=grown[:], scalar1=EXP_CAP, scalar2=None, op0=ALU.min)
-        old_picked = sb.tile([P, SLOTS], F32, name="old_picked", tag="score1")
-        nc.vector.tensor_copy(out=old_picked[:], in_=old_sb[:].indirect(list_old[:]))
-        gap = sb.tile([P, SLOTS], F32, name="gap")
+        nc.vector.tensor_tensor(out=diff[:, lo], in0=a_picked[:, lo], in1=b_picked[:, lo], op=ALU.subtract)
+
+        late = sb.tile([P, SLOTS + HALF], F32, name="late", tag="k_words1", align_bytes=64)
+        gap, old_lo = late[:, :SLOTS], late[:, SLOTS:]
+        nc.vector.tensor_copy(out=old_lo, in_=old_sb[:].indirect(list_old[:, lo_list]))
         nc.vector.scalar_tensor_tensor(
-            out=gap[:], in0=diff[:], scalar=-1.0, in1=diff[:], op0=ALU.mult, op1=ALU.max
+            out=gap, in0=diff[:], scalar=-1.0, in1=diff[:], op0=ALU.mult, op1=ALU.max
         )
 
         logged = sb.tile([P, 2, SLOTS], F32, name="logged")
-        soft = sb.tile([P, 2, SLOTS], F32, name="soft")
+        soft = sb.tile([P, 2, SLOTS], F32, name="soft", tag="soft")
+        prod = sb.tile([P, SLOTS], F32, name="prod")
         for i in range(2):
             nc.scalar.activation(out=logged[:, i, :], in_=capped[:, i, :], func=ACT.Ln, bias=1.0)
-            nc.vector.tensor_tensor(out=soft[:, i, :], in0=logged[:, i, :], in1=picked[:, i, :], op=ALU.max)
-        prod = sb.tile([P, SLOTS], F32, name="prod")
-        nc.vector.tensor_tensor(out=prod[:], in0=soft[:, 0, :], in1=soft[:, 1, :], op=ALU.mult)
+        nc.vector.tensor_tensor(out=soft[:, 0, :], in0=logged[:, 0, :], in1=a_picked[:], op=ALU.max)
+        for half in (lo, hi):
+            nc.vector.tensor_tensor(out=soft[:, 1, half], in0=logged[:, 1, half], in1=b_picked[:, half], op=ALU.max)
+        for half in (lo, hi):
+            nc.vector.tensor_tensor(out=prod[:, half], in0=soft[:, 0, half], in1=soft[:, 1, half], op=ALU.mult)
 
         root = sb.tile([P, SLOTS], F32, name="root")
         weight = sb.tile([P, SLOTS], F32, name="weight")
-        for lo, hi in zip(TAIL_CUTS, TAIL_CUTS[1:]):
-            nc.scalar.activation(out=root[:, lo:hi], in_=prod[:, lo:hi], func=ACT.Sqrt, bias=0.1)
+        old_hi = sb.tile([P, HALF], F32, name="old_hi", tag="soft")
+        for half in (lo, hi):
+            nc.scalar.activation(out=root[:, half], in_=prod[:, half], func=ACT.Sqrt, bias=0.1)
+        nc.scalar.activation(out=old_hi[:], in_=old_sb[:].indirect(list_old[:, hi_list]), func=ACT.Copy)
+        for half in (lo, hi):
             nc.vector.scalar_tensor_tensor(
-                out=weight[:, lo:hi], in0=root[:, lo:hi], scalar=lam_sb[:], in1=gap[:, lo:hi],
+                out=weight[:, half], in0=root[:, half], scalar=lam_sb[:], in1=gap[:, half],
                 op0=ALU.mult, op1=ALU.subtract,
             )
+        for half, half_list, old_half in ((lo, lo_list, old_lo), (hi, hi_list, old_hi[:])):
             nc.vector.tensor_tensor(
-                out=placed[:].indirect(list_out[:, lo // 16 : hi // 16]),
-                in0=weight[:, lo:hi], in1=old_picked[:, lo:hi], op=ALU.mult,
+                out=placed[:].indirect(list_out[:, half_list]),
+                in0=weight[:, half], in1=old_half, op=ALU.mult,
             )
 
         for c in range(T // N_OUT):

@@ -30,10 +30,10 @@ def tile_attend_agreeingtwo_lean_timesold_heads_kernel(
     nc = tc.nc
     with ExitStack() as ctx:
         sb = ctx.enter_context(tc.tile_pool(name="sb", bufs=1))
-        psum = ctx.enter_context(tc.psum_pool(name="psum", bufs=1))
+        psum = ctx.enter_context(tc.psum_pool(name="psum", bufs=4))
 
         k_scales = sb.tile([P, T], U8, name="k_scales", align_bytes=64)
-        nc.gpsimd.memset(k_scales[:].bitcast(I32), 0)
+        nc.vector.memset(k_scales[:].bitcast(I32), 0)
         placed = sb.tile([P, T], F32, name="placed")
         nc.vector.memset(placed[:], 0.0)
 
@@ -47,12 +47,12 @@ def tile_attend_agreeingtwo_lean_timesold_heads_kernel(
         lam_sb = sb.tile([P, 1], F32, name="lam_sb")
 
         nc.sync.dma_start(out=q_raw[0][:], in_=query.rearrange("(p j) q -> p j q", j=PACK))
+        nc.sync.dma_start(out=q_raw[1][:], in_=query2.rearrange("(p j) q -> p j q", j=PACK))
         for quad in range(4):
             nc.sync.dma_start(
                 out=k_scales[32 * quad : 32 * quad + 4, :].bitcast(I32),
                 in_=keys_scales[0, 4 * quad : 4 * quad + 4, :].bitcast(I32),
             )
-        nc.sync.dma_start(out=q_raw[1][:], in_=query2.rearrange("(p j) q -> p j q", j=PACK))
         for h in range(2):
             nc.sync.dma_start(out=k_words[h][:].bitcast(I32), in_=keys_words[0][:, T * h : T * (h + 1)].bitcast(I32))
         nc.sync.dma_start(list_ab[:], offs)
@@ -65,13 +65,10 @@ def tile_attend_agreeingtwo_lean_timesold_heads_kernel(
         scores = []
         for i in range(2):
             woven = sb.tile([P, Q, PACK], BF16, name="woven%d" % i, align_bytes=64)
-            if i == 0:
-                nc.vector.tensor_copy(
-                    out=woven[:].rearrange("p (c i) j -> p c j i", i=4),
-                    in_=q_raw[i][:].rearrange("p j (c i) -> p c j i", i=4),
-                )
-            else:
-                nc.scalar.copy(out=woven[:], in_=q_raw[i][:].rearrange("p j q -> p q j"))
+            nc.vector.tensor_copy(
+                out=woven[:].rearrange("p (c i) j -> p c j i", i=4),
+                in_=q_raw[i][:].rearrange("p j (c i) -> p c j i", i=4),
+            )
             q_codes = sb.tile([P, Q], U32, name="q_codes%d" % i, align_bytes=64)
             q_scales = sb.tile([P, Q], U8, name="q_scales%d" % i, align_bytes=64)
             nc.vector.quantize_mx(
@@ -81,7 +78,7 @@ def tile_attend_agreeingtwo_lean_timesold_heads_kernel(
             )
             score = sb.tile([P, T], F32, name="score%d" % i, tag="score%d" % i)
             for c in range(T // N_MM):
-                acc = psum.tile([P, N_MM], F32, name="acc%d_%d" % (i, c))
+                acc = psum.tile([P, N_MM], F32, name="acc")
                 nc.tensor.matmul_mx(
                     out=acc[:],
                     lhsT=q_codes[:].bitcast(E4M3X4),

from contextlib import ExitStack

import concourse.mybir as mybir

D, T, SLOTS, Q = 512, 1024, 512, 128
FLOPS = 2 * 2 * D * Q * T

F32 = mybir.dt.float32
BF16 = mybir.dt.bfloat16
I32 = mybir.dt.int32
U32 = mybir.dt.uint32
U16 = mybir.dt.uint16
U8 = mybir.dt.uint8
E4M3X4 = mybir.dt.float8_e4m3fn_x4
E2M1X4 = mybir.dt.float4_e2m1fn_x4
ALU = mybir.AluOpType
ACT = mybir.ActivationFunctionType

P = 128
PACK = 4
N_MM = 256
EXP_CAP = 2.0**60
HALF = SLOTS // 2
N_OUT = 256


def tile_attend_agreeingtwo_lean_timesold_heads_kernel(
    tc, query, query2, keys_words, keys_scales, lam, old, base, offs, offs2, offs3, out
):
    nc = tc.nc
    with ExitStack() as ctx:
        sb = ctx.enter_context(tc.tile_pool(name="sb", bufs=1))
        psum = ctx.enter_context(tc.psum_pool(name="psum", bufs=4))

        k_scales = sb.tile([P, T], U8, name="k_scales", align_bytes=64)
        nc.vector.memset(k_scales[:].bitcast(I32), 0)
        placed = sb.tile([P, T], F32, name="placed")
        nc.vector.memset(placed[:], 0.0)

        q_raw = [sb.tile([P, PACK, Q], F32, name="q_raw%d" % i) for i in range(2)]
        k_words = [sb.tile([P, T], U8, name="k_words%d" % h, tag="k_words%d" % h, align_bytes=64) for h in range(2)]
        list_ab = sb.tile([P, SLOTS // 16], U16, name="list_ab")
        list_old = sb.tile([P, SLOTS // 16], U16, name="list_old")
        list_out = sb.tile([P, SLOTS // 16], U16, name="list_out")
        old_sb = sb.tile([P, T], F32, name="old_sb")
        base_sb = sb.tile([P, T], F32, name="base_sb")
        lam_sb = sb.tile([P, 1], F32, name="lam_sb")

        nc.sync.dma_start(out=q_raw[0][:], in_=query.rearrange("(p j) q -> p j q", j=PACK))
        nc.sync.dma_start(out=q_raw[1][:], in_=query2.rearrange("(p j) q -> p j q", j=PACK))
        for quad in range(4):
            nc.sync.dma_start(
                out=k_scales[32 * quad : 32 * quad + 4, :].bitcast(I32),
                in_=keys_scales[0, 4 * quad : 4 * quad + 4, :].bitcast(I32),
            )
        for h in range(2):
            nc.sync.dma_start(out=k_words[h][:].bitcast(I32), in_=keys_words[0][:, T * h : T * (h + 1)].bitcast(I32))
        nc.sync.dma_start(list_ab[:], offs)
        nc.sync.dma_start(out=old_sb[:], in_=old)
        nc.sync.dma_start(list_old[:], offs2)
        nc.sync.dma_start(list_out[:], offs3)
        nc.sync.dma_start(out=lam_sb[:], in_=lam)
        nc.sync.dma_start(out=base_sb[:], in_=base)

        scores = []
        for i in range(2):
            woven = sb.tile([P, Q, PACK], BF16, name="woven%d" % i, align_bytes=64)
            nc.vector.tensor_copy(
                out=woven[:].rearrange("p (c i) j -> p c j i", i=4),
                in_=q_raw[i][:].rearrange("p j (c i) -> p c j i", i=4),
            )
            q_codes = sb.tile([P, Q], U32, name="q_codes%d" % i, align_bytes=64)
            q_scales = sb.tile([P, Q], U8, name="q_scales%d" % i, align_bytes=64)
            nc.vector.quantize_mx(
                out=q_codes[:].bitcast(E4M3X4),
                scales=q_scales[:],
                in_=woven[:].rearrange("p q j -> p (q j)"),
            )
            score = sb.tile([P, T], F32, name="score%d" % i, tag="score%d" % i)
            for c in range(T // N_MM):
                acc = psum.tile([P, N_MM], F32, name="acc")
                nc.tensor.matmul_mx(
                    out=acc[:],
                    lhsT=q_codes[:].bitcast(E4M3X4),
                    lhsT_scale=q_scales[:],
                    rhs=k_words[c // 2][:, 2 * N_MM * (c % 2) : 2 * N_MM * (c % 2 + 1)].bitcast(E2M1X4),
                    rhs_scale=k_scales[:, N_MM * c : N_MM * (c + 1)],
                    start=True,
                    stop=True,
                )
                nc.scalar.copy(out=score[:, N_MM * c : N_MM * (c + 1)], in_=acc[:])
            scores.append(score)

        a_all, b_all = scores
        lo, hi = slice(0, HALF), slice(HALF, SLOTS)
        lo_list, hi_list = slice(0, HALF // 16), slice(HALF // 16, SLOTS // 16)

        a_picked = sb.tile([P, SLOTS], F32, name="a_picked")
        b_picked = sb.tile([P, SLOTS], F32, name="b_picked")
        nc.vector.tensor_copy(out=a_picked[:, lo], in_=a_all[:].indirect(list_ab[:, lo_list]))
        nc.vector.tensor_copy(out=a_picked[:, hi], in_=a_all[:].indirect(list_ab[:, hi_list]))
        nc.vector.tensor_copy(out=b_picked[:, hi], in_=b_all[:].indirect(list_ab[:, hi_list]))
        nc.vector.tensor_copy(out=b_picked[:, lo], in_=b_all[:].indirect(list_ab[:, lo_list]))

        grown = sb.tile([P, 2, SLOTS], F32, name="grown", tag="k_words1", align_bytes=64)
        nc.scalar.activation(out=grown[:, 0, lo], in_=a_picked[:, lo], func=ACT.Exp)
        nc.scalar.activation(out=grown[:, 1, lo], in_=b_all[:].indirect(list_ab[:, lo_list]), func=ACT.Exp)
        nc.scalar.activation(out=grown[:, 0, hi], in_=a_picked[:, hi], func=ACT.Exp)
        nc.scalar.activation(out=grown[:, 1, hi], in_=b_picked[:, hi], func=ACT.Exp)

        diff = sb.tile([P, SLOTS], F32, name="diff")
        capped = sb.tile([P, 2, SLOTS], F32, name="capped")
        nc.vector.tensor_tensor(out=diff[:, hi], in0=a_picked[:, hi], in1=b_picked[:, hi], op=ALU.subtract)
        nc.vector.tensor_scalar(out=capped[:], in0=grown[:], scalar1=EXP_CAP, scalar2=None, op0=ALU.min)
        nc.vector.tensor_tensor(out=diff[:, lo], in0=a_picked[:, lo], in1=b_picked[:, lo], op=ALU.subtract)

        late = sb.tile([P, SLOTS + HALF], F32, name="late", tag="k_words1", align_bytes=64)
        gap, old_lo = late[:, :SLOTS], late[:, SLOTS:]
        nc.vector.tensor_copy(out=old_lo, in_=old_sb[:].indirect(list_old[:, lo_list]))
        nc.vector.scalar_tensor_tensor(
            out=gap, in0=diff[:], scalar=-1.0, in1=diff[:], op0=ALU.mult, op1=ALU.max
        )

        logged = sb.tile([P, 2, SLOTS], F32, name="logged")
        soft = sb.tile([P, 2, SLOTS], F32, name="soft", tag="soft")
        prod = sb.tile([P, SLOTS], F32, name="prod")
        for i in range(2):
            nc.scalar.activation(out=logged[:, i, :], in_=capped[:, i, :], func=ACT.Ln, bias=1.0)
        nc.vector.tensor_tensor(out=soft[:, 0, :], in0=logged[:, 0, :], in1=a_picked[:], op=ALU.max)
        for half in (lo, hi):
            nc.vector.tensor_tensor(out=soft[:, 1, half], in0=logged[:, 1, half], in1=b_picked[:, half], op=ALU.max)
        for half in (lo, hi):
            nc.vector.tensor_tensor(out=prod[:, half], in0=soft[:, 0, half], in1=soft[:, 1, half], op=ALU.mult)

        root = sb.tile([P, SLOTS], F32, name="root")
        weight = sb.tile([P, SLOTS], F32, name="weight")
        old_hi = sb.tile([P, HALF], F32, name="old_hi", tag="soft")
        for half in (lo, hi):
            nc.scalar.activation(out=root[:, half], in_=prod[:, half], func=ACT.Sqrt, bias=0.1)
        nc.scalar.activation(out=old_hi[:], in_=old_sb[:].indirect(list_old[:, hi_list]), func=ACT.Copy)
        for half in (lo, hi):
            nc.vector.scalar_tensor_tensor(
                out=weight[:, half], in0=root[:, half], scalar=lam_sb[:], in1=gap[:, half],
                op0=ALU.mult, op1=ALU.subtract,
            )
        for half, half_list, old_half in ((lo, lo_list, old_lo), (hi, hi_list, old_hi[:])):
            nc.vector.tensor_tensor(
                out=placed[:].indirect(list_out[:, half_list]),
                in0=weight[:, half], in1=old_half, op=ALU.mult,
            )

        for c in range(T // N_OUT):
            cols = slice(N_OUT * c, N_OUT * (c + 1))
            result = sb.tile([P, N_OUT], F32, name="result%d" % c)
            nc.vector.tensor_tensor(out=result[:], in0=placed[:, cols], in1=base_sb[:, cols], op=ALU.add)
            queue = nc.sync if c % 2 == 0 else nc.scalar
            queue.dma_start(out=out[:, cols], in_=result[:])
